import numpy as np
import ml_dtypes


def mxq(x, axis, fmt="e4m3"):
    dtype, down = {"e4m3": (ml_dtypes.float8_e4m3fn, 7), "e5m2": (ml_dtypes.float8_e5m2, 14)}[fmt]
    v = np.moveaxis(np.asarray(x, np.float32).astype(ml_dtypes.bfloat16).astype(np.float64), axis, -1)
    blocks = v.reshape(v.shape[:-1] + (-1, 32))
    amax = np.abs(blocks).max(-1, keepdims=True)
    byte = np.maximum(np.where(amax > 0, np.frexp(amax)[1] - 1 + 127, 0) - down, 1)
    scale = np.exp2(byte - 127.0)
    codes = (blocks / scale).astype(np.float32).astype(dtype).astype(np.float64)
    return np.moveaxis((codes * scale).reshape(v.shape), -1, axis)


WIDE = False


def mx_kscale(k):
    if not WIDE:
        return np.ones(k)
    levels = np.array([30, -30])
    if k % 512:
        return np.exp2(np.random.permutation(np.resize(levels, k // 32))).repeat(32)
    a = np.empty((k // 512, 16))
    for p in range(k // 512):
        a[p, :8] = np.random.permutation(np.resize(levels, 8))
        for g in range(8):
            far = levels[np.abs(levels - a[p, g]) >= 10]
            a[p, g + 8] = far[np.random.randint(len(far))]
    return np.exp2(a.ravel()).repeat(32)


def f64(x):
    return np.asarray(x).astype(np.float64)


def striped(idx):
    return np.tile(np.asarray(idx).reshape(-1, 16).T, (8, 1)).astype(np.uint16)


def unstriped(offs):
    return offs[:16].T.reshape(-1).astype(np.int64)


E2M1 = np.array([0.0, 0.5, 1.0, 1.5, 2.0, 3.0, 4.0, 6.0, -0.0, -0.5, -1.0, -1.5, -2.0, -3.0, -4.0, -6.0])


def pack_weight(w, fmt):
    k, n = w.shape
    w = f64(np.asarray(w, np.float32).astype(ml_dtypes.bfloat16)).reshape(k // 32, 32, n)
    amax = np.abs(w).max(1)
    if fmt in ("e4m3", "e5m2"):
        byte = np.frexp(amax)[1] - 1 + 127 - (7 if fmt == "e4m3" else 14)
    else:
        mant, ex = np.frexp(amax / 6.0)
        byte = np.where(mant > 0.5, ex, ex - 1) + 127
    byte = np.clip(np.where(amax > 0, byte, 1), 1, 254)
    scaled = (w * np.exp2(127.0 - byte)[:, None, :]).reshape(k, n).astype(np.float32)
    by_word = np.ascontiguousarray(scaled.reshape(k // 512, 128, 4, n).transpose(0, 1, 3, 2))
    if fmt in ("e4m3", "e5m2"):
        words = by_word.astype(ml_dtypes.float8_e4m3fn if fmt == "e4m3" else ml_dtypes.float8_e5m2).view(np.uint8)
    else:
        c = by_word.astype(ml_dtypes.float4_e2m1fn).view(np.uint8) & 0xF
        words = (c[..., 0::2] | (c[..., 1::2] << 4)).reshape(k // 512, 128, 2 * n)
    return np.ascontiguousarray(words), np.ascontiguousarray(byte.astype(np.uint8).reshape(k // 512, 16, n))


def unpack_weight(words, scales, fmt):
    g, _, n = scales.shape
    words = np.ascontiguousarray(words).reshape(g, 128, n, -1)
    if fmt in ("e4m3", "e5m2"):
        vals = words.view(ml_dtypes.float8_e4m3fn if fmt == "e4m3" else ml_dtypes.float8_e5m2).astype(np.float64)
    else:
        nib = np.empty((g, 128, n, 4), np.uint8)
        nib[..., 0::2] = words & 0xF
        nib[..., 1::2] = words >> 4
        vals = E2M1[nib]
    vals = vals * np.repeat(np.exp2(scales.astype(np.float64) - 127.0), 8, axis=1)[..., None]
    return vals.transpose(0, 1, 3, 2).reshape(g * 512, n)


K, T, J, I, R, C, G, Q = 512, 512, 256, 256, 512, 512, 32, 512


def setup_inputs():
    n = np.random.standard_normal
    idx = np.random.permutation(T)[:J]
    idx2 = np.random.permutation(C)[:J]
    idx3 = np.random.permutation(T)[:I]
    idx4 = np.random.permutation(Q)[:I]
    fk = mx_kscale(K)
    fr = mx_kscale(R)
    xtp = pack_weight(n((K, T)) / fk[:, None], "e4m3")
    wap = pack_weight(n((K, R)) * 0.5 / np.sqrt(K) * fk[:, None] * fr, "e5m2")
    wbp = pack_weight(n((K, R)) * 1 / np.sqrt(K) * fk[:, None] / fr, "e2m1")
    return {
        "xt_words": xtp[0],
        "xt_scales": xtp[1],
        "wa_words": wap[0],
        "wa_scales": wap[1],
        "tf": (n((R, C))).astype(np.float32),
        "wb_words": wbp[0],
        "wb_scales": wbp[1],
        "tv": (1.0 * n((J, Q))).astype(np.float32),
        "offs": striped(idx),
        "offs2": striped(idx2),
        "offs3": striped(idx3),
        "offs4": striped(idx4),
    }


def reference(xt_words, xt_scales, wa_words, wa_scales, tf, wb_words, wb_scales, tv, offs, offs2, offs3, offs4):
    idx = unstriped(offs)
    idx2 = unstriped(offs2)
    idx3 = unstriped(offs3)
    idx4 = unstriped(offs4)
    xtu = unpack_weight(xt_words, xt_scales, "e4m3")
    wau = unpack_weight(wa_words, wa_scales, "e5m2")
    wbu = unpack_weight(wb_words, wb_scales, "e2m1")
    xtidxg = xtu[:, idx]
    za = wau.T @ xtidxg
    ha = za * f64(tf)[:, idx2]
    xtidx3g = xtu[:, idx3]
    zb = wbu.T @ xtidx3g
    mb1 = zb.reshape(R, G, I // G).mean(axis=2)
    mb2 = np.repeat(mb1, I // G, axis=1)
    hb = zb - mb2
    haq = mxq(ha, 0, "e4m3")
    hbq = mxq(hb, 0, "e5m2")
    a0 = haq.T @ hbq
    y = np.tanh(0.04 * a0) * f64(tv)[:, idx4]
    return y

@@ -1,0 +1,198 @@
+from contextlib import ExitStack
+
+import concourse.mybir as mybir
+
+K, T, J, I, R, C, Q = 512, 512, 256, 256, 512, 512, 512
+FLOPS = 2 * K * R * J + 2 * K * R * I + 2 * R * J * I
+
+F32 = mybir.dt.float32
+BF16 = mybir.dt.bfloat16
+I32 = mybir.dt.int32
+U32 = mybir.dt.uint32
+U16 = mybir.dt.uint16
+U8 = mybir.dt.uint8
+E4M3 = mybir.dt.float8_e4m3fn_x4
+E5M2 = mybir.dt.float8_e5m2_x4
+E2M1 = mybir.dt.float4_e2m1fn_x4
+ALU = mybir.AluOpType
+ACT = mybir.ActivationFunctionType
+
+P = 128
+PACK = 4
+RUN = 8
+BUNDLE = 8
+HALF = 128
+
+
+def load_scale_rows(engine, plane, scales, quadrant):
+    engine.dma_start(
+        out=plane[32 * quadrant : 32 * quadrant + 4, :].bitcast(I32),
+        in_=scales[0, 4 * quadrant : 4 * quadrant + 4, :].bitcast(I32),
+    )
+
+
+def tile_list_meet_timestable_levelled_tabled_kernel(
+    tc, xt_words, xt_scales, wa_words, wa_scales, tf, wb_words, wb_scales, tv, offs, offs2, offs3, offs4, out
+):
+    nc = tc.nc
+    with ExitStack() as ctx:
+        sb = ctx.enter_context(tc.tile_pool(name="sb", bufs=1))
+        ps = ctx.enter_context(tc.psum_pool(name="ps", bufs=1))
+
+        list_a = sb.tile([P, J // 16], U16, name="list_a")
+        list_f = sb.tile([P, J // 16], U16, name="list_f")
+        list_b = sb.tile([P, I // 16], U16, name="list_b")
+        list_v = sb.tile([P, I // 16], U16, name="list_v")
+        xt_w = sb.tile([P, T], U32, name="xt_w", align_bytes=64)
+        xt_s = sb.tile([P, T], U8, name="xt_s", align_bytes=64)
+        wa_w_raw = sb.tile([P, R], U32, name="wa_w_raw", align_bytes=64)
+        wa_s_raw = sb.tile([P, R], U8, name="wa_s_raw", align_bytes=64)
+        wb_w_raw = sb.tile([P, 2 * R], U8, name="wb_w_raw", align_bytes=64)
+        wb_s_raw = sb.tile([P, R], U8, name="wb_s_raw", align_bytes=64)
+        tf_rows = [sb.tile([P, C], F32, name="tf_rows%d" % t) for t in range(PACK)]
+        tv_rows = sb.tile([P, J // P, Q], F32, name="tv_rows")
+
+        nc.vector.memset(xt_s[:].bitcast(I32), 0)
+        nc.vector.memset(wb_s_raw[:].bitcast(I32), 0)
+        nc.vector.memset(wa_s_raw[:].bitcast(I32), 0)
+
+        nc.sync.dma_start(list_b[:], offs3)
+        nc.scalar.dma_start(
+            out=xt_w[:].bitcast(I32), in_=xt_words[0].rearrange("p c r -> p (c r)").bitcast(I32)
+        )
+        load_scale_rows(nc.sync, xt_s, xt_scales, 0)
+        load_scale_rows(nc.scalar, xt_s, xt_scales, 1)
+        load_scale_rows(nc.sync, xt_s, xt_scales, 2)
+        load_scale_rows(nc.scalar, xt_s, xt_scales, 3)
+        nc.sync.dma_start(list_a[:], offs)
+        nc.scalar.dma_start(out=wb_w_raw[:].bitcast(I32), in_=wb_words[0].bitcast(I32))
+        for quadrant in range(4):
+            load_scale_rows(nc.sync, wb_s_raw, wb_scales, quadrant)
+        nc.sync.dma_start(
+            out=wa_w_raw[:].bitcast(I32), in_=wa_words[0].rearrange("p c r -> p (c r)").bitcast(I32)
+        )
+        nc.sync.dma_start(list_f[:], offs2)
+        tf_dealt = tf.rearrange("(b t u) c -> t b u c", t=PACK, u=RUN)
+        for t in range(PACK):
+            nc.sync.dma_start(out=tf_rows[t][:], in_=tf_dealt[t])
+        for quadrant in range(4):
+            load_scale_rows(nc.sync, wa_s_raw, wa_scales, quadrant)
+        nc.sync.dma_start(out=tv_rows[:], in_=tv.rearrange("(h p) q -> p h q", p=P))
+        nc.sync.dma_start(list_v[:], offs4)
+
+        xb_w = sb.tile([P, I], U32, name="xb_w", align_bytes=64)
+        xb_s = sb.tile([P, I], U8, name="xb_s", align_bytes=64)
+        xa_w = sb.tile([P, J], U32, name="xa_w", align_bytes=64)
+        xa_s = sb.tile([P, J], U8, name="xa_s", align_bytes=64)
+        nc.vector.tensor_copy(xb_w[:], xt_w[:].indirect(list_b[:]))
+        nc.vector.tensor_copy(xb_s[:], xt_s[:].indirect(list_b[:]))
+        nc.vector.tensor_copy(xa_w[:], xt_w[:].indirect(list_a[:]))
+        nc.vector.tensor_copy(xa_s[:], xt_s[:].indirect(list_a[:]))
+
+        wb_w = sb.tile([P, 2 * R], U8, name="wb_w", align_bytes=64)
+        wb_s = sb.tile([P, R], U8, name="wb_s", align_bytes=64)
+        wa_w = sb.tile([P, R], U32, name="wa_w", align_bytes=64)
+        wa_s = sb.tile([P, R], U8, name="wa_s", align_bytes=64)
+
+        def deal(dst, src):
+            nc.scalar.copy(
+                out=dst[:].bitcast(U32).rearrange("p (t b w) -> p t b w", t=PACK, b=R // 32),
+                in_=src[:].bitcast(U32).rearrange("p (b t w) -> p t b w", t=PACK, b=R // 32),
+            )
+
+        def first_stage(name, w, w_dtype, bytes_per_column, s, x_w, x_s):
+            banks = [ps.tile([P, PACK, HALF], F32, name="%s%d" % (name, h)) for h in range(2)]
+            for h in range(2):
+                cols = slice(h * HALF, (h + 1) * HALF)
+                for t in range(PACK):
+                    nc.tensor.matmul_mx(
+                        out=banks[h][:, t, :],
+                        lhsT=w[:, t * P * bytes_per_column : (t + 1) * P * bytes_per_column].bitcast(w_dtype),
+                        lhsT_scale=s[:, t * P : (t + 1) * P],
+                        rhs=x_w[:, cols].bitcast(E4M3),
+                        rhs_scale=x_s[:, cols],
+                        start=True,
+                        stop=True,
+                    )
+            return banks
+
+        deal(wb_w, wb_w_raw)
+        deal(wb_s, wb_s_raw)
+        zb = first_stage("zb", wb_w, E2M1, 2, wb_s, xb_w, xb_s)
+        deal(wa_w, wa_w_raw)
+        deal(wa_s, wa_s_raw)
+        za = first_stage("za", wa_w, E5M2, 1, wa_s, xa_w, xa_s)
+
+        tf_g = sb.tile([P, PACK, J], F32, name="tf_g")
+        for t in range(PACK):
+            nc.scalar.activation(tf_g[:, t, :], tf_rows[t][:].indirect(list_f[:]), ACT.Copy)
+        tv_g = [sb.tile([P, I], F32, name="tv_g%d" % h) for h in range(2)]
+        for h in range(2):
+            nc.scalar.activation(tv_g[h][:], tv_rows[:, h, :].indirect(list_v[:]), ACT.Copy)
+
+        groups = HALF // BUNDLE
+        sums = [sb.tile([P, groups, PACK], F32, name="sums%d" % h) for h in range(2)]
+        means = [sb.tile([P, groups, PACK], F32, name="means%d" % h) for h in range(2)]
+        hb = sb.tile([P, I, PACK], BF16, name="hb", align_bytes=64)
+        for h in range(2):
+            nc.vector.tensor_reduce(
+                out=sums[h][:],
+                in_=zb[h][:].rearrange("p t (g u) -> p g t u", u=BUNDLE),
+                axis=mybir.AxisListType.X,
+                op=ALU.add,
+            )
+        for h in range(2):
+            nc.vector.tensor_scalar(
+                out=means[h][:], in0=sums[h][:], scalar1=1.0 / BUNDLE, scalar2=None, op0=ALU.mult
+            )
+        for h in range(2):
+            nc.vector.tensor_tensor(
+                out=hb[:, h * HALF : (h + 1) * HALF, :].rearrange("p (g u) t -> p g u t", u=BUNDLE),
+                in0=zb[h][:].rearrange("p t (g u) -> p g u t", u=BUNDLE),
+                in1=means[h][:].unsqueeze(2).to_broadcast([P, groups, BUNDLE, PACK]),
+                op=ALU.subtract,
+            )
+
+        ha = [sb.tile([P, HALF, PACK], BF16, name="ha%d" % h, align_bytes=64) for h in range(2)]
+        ha_w = [sb.tile([P, HALF], U32, name="ha_w%d" % h, align_bytes=64) for h in range(2)]
+        ha_s = [sb.tile([P, HALF], U8, name="ha_s%d" % h, align_bytes=64) for h in range(2)]
+        hb_w = sb.tile([P, I], U32, name="hb_w", align_bytes=64)
+        hb_s = sb.tile([P, I], U8, name="hb_s", align_bytes=64)
+
+        def scale_rows(h):
+            nc.vector.tensor_tensor(
+                out=ha[h][:].rearrange("p (c i) t -> p c t i", i=4),
+                in0=za[h][:].rearrange("p t (c i) -> p c t i", i=4),
+                in1=tf_g[:, :, h * HALF : (h + 1) * HALF].rearrange("p t (c i) -> p c t i", i=4),
+                op=ALU.mult,
+            )
+
+        def quantize_rows(h):
+            nc.vector.quantize_mx(
+                out=ha_w[h][:].bitcast(E4M3), scales=ha_s[h][:], in_=ha[h][:].rearrange("p j t -> p (j t)")
+            )
+
+        scale_rows(0)
+        nc.vector.quantize_mx(
+            out=hb_w[:].bitcast(E5M2), scales=hb_s[:], in_=hb[:].rearrange("p i t -> p (i t)")
+        )
+        quantize_rows(0)
+        scale_rows(1)
+        quantize_rows(1)
+
+        for h in range(2):
+            scores = ps.tile([P, I], F32, name="scores%d" % h)
+            nc.tensor.matmul_mx(
+                out=scores[:],
+                lhsT=ha_w[h][:].bitcast(E4M3),
+                lhsT_scale=ha_s[h][:],
+                rhs=hb_w[:].bitcast(E5M2),
+                rhs_scale=hb_s[:],
+                start=True,
+                stop=True,
+            )
+            squashed = sb.tile([P, I], F32, name="squashed%d" % h)
+            nc.scalar.activation(squashed[:], scores[:], ACT.Tanh, scale=0.04)
+            result = sb.tile([P, I], F32, name="result%d" % h)
+            nc.vector.tensor_tensor(out=result[:], in0=squashed[:], in1=tv_g[h][:], op=ALU.mult)
+            nc.sync.dma_start(out=out[h * P : (h + 1) * P, :], in_=result[:])

@@ -26,8 +26,8 @@ HALF = 128
 
 def load_scale_rows(engine, plane, scales, quadrant):
     engine.dma_start(
-        out=plane[32 * quadrant : 32 * quadrant + 4, :].bitcast(I32),
-        in_=scales[0, 4 * quadrant : 4 * quadrant + 4, :].bitcast(I32),
+        out=plane[32 * quadrant : 32 * quadrant + 32, :].bitcast(I32),
+        in_=scales[0, 4 * quadrant : 4 * quadrant + 4, :].bitcast(I32).partition_broadcast(8),
     )
 
 
@@ -52,28 +52,25 @@ def tile_list_meet_timestable_levelled_tabled_kernel(
         tf_rows = [sb.tile([P, C], F32, name="tf_rows%d" % t) for t in range(PACK)]
         tv_rows = sb.tile([P, J // P, Q], F32, name="tv_rows")
 
-        nc.vector.memset(xt_s[:].bitcast(I32), 0)
-        nc.vector.memset(wb_s_raw[:].bitcast(I32), 0)
-        nc.vector.memset(wa_s_raw[:].bitcast(I32), 0)
 
         nc.sync.dma_start(list_b[:], offs3)
+        tf_dealt = tf.rearrange("(b t u) c -> t b u c", t=PACK, u=RUN)
+        for quadrant in range(4):
+            load_scale_rows(nc.sync if quadrant % 2 else nc.scalar, xt_s, xt_scales, quadrant)
+        nc.scalar.dma_start(out=wb_w_raw[:].bitcast(I32), in_=wb_words[0].bitcast(I32))
+        nc.sync.dma_start(list_f[:], offs2)
         nc.scalar.dma_start(
             out=xt_w[:].bitcast(I32), in_=xt_words[0].rearrange("p c r -> p (c r)").bitcast(I32)
         )
-        load_scale_rows(nc.sync, xt_s, xt_scales, 0)
-        load_scale_rows(nc.scalar, xt_s, xt_scales, 1)
-        load_scale_rows(nc.sync, xt_s, xt_scales, 2)
-        load_scale_rows(nc.scalar, xt_s, xt_scales, 3)
-        nc.sync.dma_start(list_a[:], offs)
-        nc.scalar.dma_start(out=wb_w_raw[:].bitcast(I32), in_=wb_words[0].bitcast(I32))
+        for t in range(2):
+            nc.gpsimd.dma_start(out=tf_rows[t][:], in_=tf_dealt[t])
         for quadrant in range(4):
             load_scale_rows(nc.sync, wb_s_raw, wb_scales, quadrant)
+        nc.sync.dma_start(list_a[:], offs)
         nc.sync.dma_start(
             out=wa_w_raw[:].bitcast(I32), in_=wa_words[0].rearrange("p c r -> p (c r)").bitcast(I32)
         )
-        nc.sync.dma_start(list_f[:], offs2)
-        tf_dealt = tf.rearrange("(b t u) c -> t b u c", t=PACK, u=RUN)
-        for t in range(PACK):
+        for t in range(2, PACK):
             nc.sync.dma_start(out=tf_rows[t][:], in_=tf_dealt[t])
         for quadrant in range(4):
             load_scale_rows(nc.sync, wa_s_raw, wa_scales, quadrant)
@@ -84,18 +81,14 @@ def tile_list_meet_timestable_levelled_tabled_kernel(
         xb_s = sb.tile([P, I], U8, name="xb_s", align_bytes=64)
         xa_w = sb.tile([P, J], U32, name="xa_w", align_bytes=64)
         xa_s = sb.tile([P, J], U8, name="xa_s", align_bytes=64)
-        nc.vector.tensor_copy(xb_w[:], xt_w[:].indirect(list_b[:]))
-        nc.vector.tensor_copy(xb_s[:], xt_s[:].indirect(list_b[:]))
-        nc.vector.tensor_copy(xa_w[:], xt_w[:].indirect(list_a[:]))
-        nc.vector.tensor_copy(xa_s[:], xt_s[:].indirect(list_a[:]))
 
         wb_w = sb.tile([P, 2 * R], U8, name="wb_w", align_bytes=64)
         wb_s = sb.tile([P, R], U8, name="wb_s", align_bytes=64)
         wa_w = sb.tile([P, R], U32, name="wa_w", align_bytes=64)
         wa_s = sb.tile([P, R], U8, name="wa_s", align_bytes=64)
 
-        def deal(dst, src):
-            nc.scalar.copy(
+        def deal(copy, dst, src):
+            copy(
                 out=dst[:].bitcast(U32).rearrange("p (t b w) -> p t b w", t=PACK, b=R // 32),
                 in_=src[:].bitcast(U32).rearrange("p (b t w) -> p t b w", t=PACK, b=R // 32),
             )
@@ -116,12 +109,14 @@ def tile_list_meet_timestable_levelled_tabled_kernel(
                     )
             return banks
 
-        deal(wb_w, wb_w_raw)
-        deal(wb_s, wb_s_raw)
+        nc.vector.tensor_copy(xb_s[:], xt_s[:].indirect(list_b[:]))
+        nc.vector.tensor_copy(xb_w[:], xt_w[:].indirect(list_b[:]))
+        deal(nc.scalar.copy, wb_w, wb_w_raw)
+        deal(nc.vector.tensor_copy, wb_s, wb_s_raw)
+        nc.vector.tensor_copy(xa_w[:], xt_w[:].indirect(list_a[:]))
+        nc.vector.tensor_copy(xa_s[:], xt_s[:].indirect(list_a[:]))
         zb = first_stage("zb", wb_w, E2M1, 2, wb_s, xb_w, xb_s)
-        deal(wa_w, wa_w_raw)
-        deal(wa_s, wa_s_raw)
-        za = first_stage("za", wa_w, E5M2, 1, wa_s, xa_w, xa_s)
+        deal(nc.scalar.copy, wa_w, wa_w_raw)
 
         tf_g = sb.tile([P, PACK, J], F32, name="tf_g")
         for t in range(PACK):
@@ -141,10 +136,16 @@ def tile_list_meet_timestable_levelled_tabled_kernel(
                 axis=mybir.AxisListType.X,
                 op=ALU.add,
             )
-        for h in range(2):
-            nc.vector.tensor_scalar(
-                out=means[h][:], in0=sums[h][:], scalar1=1.0 / BUNDLE, scalar2=None, op0=ALU.mult
+
+        def take_mean(h):
+            nc.gpsimd.tensor_scalar(
+                out=means[h][:], in0=sums[h][:], scalar1=1.0 / BUNDLE, scalar2=0.0, op0=ALU.mult, op1=ALU.add
             )
+
+        take_mean(0)
+        take_mean(1)
+        deal(nc.gpsimd.tensor_copy, wa_s, wa_s_raw)
+        za = first_stage("za", wa_w, E5M2, 1, wa_s, xa_w, xa_s)
         for h in range(2):
             nc.vector.tensor_tensor(
                 out=hb[:, h * HALF : (h + 1) * HALF, :].rearrange("p (g u) t -> p g u t", u=BUNDLE),
@@ -172,27 +173,36 @@ def tile_list_meet_timestable_levelled_tabled_kernel(
                 out=ha_w[h][:].bitcast(E4M3), scales=ha_s[h][:], in_=ha[h][:].rearrange("p j t -> p (j t)")
             )
 
+        def quantize_columns(h):
+            cols = slice(h * HALF, (h + 1) * HALF)
+            nc.vector.quantize_mx(
+                out=hb_w[:, cols].bitcast(E5M2),
+                scales=hb_s[:, cols],
+                in_=hb[:, cols, :].rearrange("p i t -> p (i t)"),
+            )
+
+        quantize_columns(0)
         scale_rows(0)
-        nc.vector.quantize_mx(
-            out=hb_w[:].bitcast(E5M2), scales=hb_s[:], in_=hb[:].rearrange("p i t -> p (i t)")
-        )
+        quantize_columns(1)
         quantize_rows(0)
         scale_rows(1)
         quantize_rows(1)
 
         for h in range(2):
-            scores = ps.tile([P, I], F32, name="scores%d" % h)
-            nc.tensor.matmul_mx(
-                out=scores[:],
-                lhsT=ha_w[h][:].bitcast(E4M3),
-                lhsT_scale=ha_s[h][:],
-                rhs=hb_w[:].bitcast(E5M2),
-                rhs_scale=hb_s[:],
-                start=True,
-                stop=True,
-            )
-            squashed = sb.tile([P, I], F32, name="squashed%d" % h)
-            nc.scalar.activation(squashed[:], scores[:], ACT.Tanh, scale=0.04)
-            result = sb.tile([P, I], F32, name="result%d" % h)
-            nc.vector.tensor_tensor(out=result[:], in0=squashed[:], in1=tv_g[h][:], op=ALU.mult)
-            nc.sync.dma_start(out=out[h * P : (h + 1) * P, :], in_=result[:])
+            for c in range(2):
+                cols = slice(c * HALF, (c + 1) * HALF)
+                scores = ps.tile([P, HALF], F32, name="scores%d%d" % (h, c))
+                nc.tensor.matmul_mx(
+                    out=scores[:],
+                    lhsT=ha_w[h][:].bitcast(E4M3),
+                    lhsT_scale=ha_s[h][:],
+                    rhs=hb_w[:, cols].bitcast(E5M2),
+                    rhs_scale=hb_s[:, cols],
+                    start=True,
+                    stop=True,
+                )
+                squashed = sb.tile([P, HALF], F32, name="squashed%d%d" % (h, c))
+                nc.scalar.activation(squashed[:], scores[:], ACT.Tanh, scale=0.04)
+                result = sb.tile([P, HALF], F32, name="result%d%d" % (h, c))
+                nc.vector.tensor_tensor(out=result[:], in0=squashed[:], in1=tv_g[h][:, cols], op=ALU.mult)
+                nc.sync.dma_start(out=out[h * P : (h + 1) * P, cols], in_=result[:])

@@ -26,8 +26,8 @@ HALF = 128
 
 def load_scale_rows(engine, plane, scales, quadrant):
     engine.dma_start(
-        out=plane[32 * quadrant : 32 * quadrant + 32, :].bitcast(I32),
-        in_=scales[0, 4 * quadrant : 4 * quadrant + 4, :].bitcast(I32).partition_broadcast(8),
+        out=plane[32 * quadrant : 32 * quadrant + 4, :].bitcast(I32),
+        in_=scales[0, 4 * quadrant : 4 * quadrant + 4, :].bitcast(I32),
     )
 
 
@@ -53,20 +53,23 @@ def tile_list_meet_timestable_levelled_tabled_kernel(
         tv_rows = sb.tile([P, J // P, Q], F32, name="tv_rows")
 
 
+        for plane in (xt_s, wb_s_raw, wa_s_raw):
+            nc.vector.memset(plane[:].bitcast(I32), 0)
+
         nc.sync.dma_start(list_b[:], offs3)
+        nc.scalar.dma_start(out=wb_w_raw[:].bitcast(I32), in_=wb_words[0].bitcast(I32))
+        nc.sync.dma_start(list_a[:], offs)
         tf_dealt = tf.rearrange("(b t u) c -> t b u c", t=PACK, u=RUN)
         for quadrant in range(4):
             load_scale_rows(nc.sync if quadrant % 2 else nc.scalar, xt_s, xt_scales, quadrant)
-        nc.scalar.dma_start(out=wb_w_raw[:].bitcast(I32), in_=wb_words[0].bitcast(I32))
-        nc.sync.dma_start(list_f[:], offs2)
         nc.scalar.dma_start(
             out=xt_w[:].bitcast(I32), in_=xt_words[0].rearrange("p c r -> p (c r)").bitcast(I32)
         )
         for t in range(2):
             nc.gpsimd.dma_start(out=tf_rows[t][:], in_=tf_dealt[t])
         for quadrant in range(4):
-            load_scale_rows(nc.sync, wb_s_raw, wb_scales, quadrant)
-        nc.sync.dma_start(list_a[:], offs)
+            load_scale_rows(nc.scalar if quadrant % 2 else nc.sync, wb_s_raw, wb_scales, quadrant)
+        nc.sync.dma_start(list_f[:], offs2)
         nc.sync.dma_start(
             out=wa_w_raw[:].bitcast(I32), in_=wa_words[0].rearrange("p c r -> p (c r)").bitcast(I32)
         )
@@ -110,11 +113,11 @@ def tile_list_meet_timestable_levelled_tabled_kernel(
             return banks
 
         nc.vector.tensor_copy(xb_s[:], xt_s[:].indirect(list_b[:]))
-        nc.vector.tensor_copy(xb_w[:], xt_w[:].indirect(list_b[:]))
-        deal(nc.scalar.copy, wb_w, wb_w_raw)
-        deal(nc.vector.tensor_copy, wb_s, wb_s_raw)
-        nc.vector.tensor_copy(xa_w[:], xt_w[:].indirect(list_a[:]))
         nc.vector.tensor_copy(xa_s[:], xt_s[:].indirect(list_a[:]))
+        nc.vector.tensor_copy(xb_w[:], xt_w[:].indirect(list_b[:]))
+        nc.vector.tensor_copy(xa_w[:], xt_w[:].indirect(list_a[:]))
+        deal(nc.scalar.copy, wb_w, wb_w_raw)
+        deal(nc.scalar.copy, wb_s, wb_s_raw)
         zb = first_stage("zb", wb_w, E2M1, 2, wb_s, xb_w, xb_s)
         deal(nc.scalar.copy, wa_w, wa_w_raw)
 

@@ -73,10 +73,10 @@ def tile_list_meet_timestable_levelled_tabled_kernel(
         nc.sync.dma_start(
             out=wa_w_raw[:].bitcast(I32), in_=wa_words[0].rearrange("p c r -> p (c r)").bitcast(I32)
         )
-        for t in range(2, PACK):
-            nc.sync.dma_start(out=tf_rows[t][:], in_=tf_dealt[t])
         for quadrant in range(4):
             load_scale_rows(nc.sync, wa_s_raw, wa_scales, quadrant)
+        for t in range(2, PACK):
+            nc.sync.dma_start(out=tf_rows[t][:], in_=tf_dealt[t])
         nc.sync.dma_start(out=tv_rows[:], in_=tv.rearrange("(h p) q -> p h q", p=P))
         nc.sync.dma_start(list_v[:], offs4)
 
@@ -146,8 +146,8 @@ def tile_list_meet_timestable_levelled_tabled_kernel(
             )
 
         take_mean(0)
-        take_mean(1)
         deal(nc.gpsimd.tensor_copy, wa_s, wa_s_raw)
+        take_mean(1)
         za = first_stage("za", wa_w, E5M2, 1, wa_s, xa_w, xa_s)
         for h in range(2):
             nc.vector.tensor_tensor(

from contextlib import ExitStack

import concourse.mybir as mybir

K, T, J, I, R, C, Q = 512, 512, 256, 256, 512, 512, 512
FLOPS = 2 * K * R * J + 2 * K * R * I + 2 * R * J * I

F32 = mybir.dt.float32
BF16 = mybir.dt.bfloat16
I32 = mybir.dt.int32
U32 = mybir.dt.uint32
U16 = mybir.dt.uint16
U8 = mybir.dt.uint8
E4M3 = mybir.dt.float8_e4m3fn_x4
E5M2 = mybir.dt.float8_e5m2_x4
E2M1 = mybir.dt.float4_e2m1fn_x4
ALU = mybir.AluOpType
ACT = mybir.ActivationFunctionType

P = 128
PACK = 4
RUN = 8
BUNDLE = 8
HALF = 128


def load_scale_rows(engine, plane, scales, quadrant):
    engine.dma_start(
        out=plane[32 * quadrant : 32 * quadrant + 4, :].bitcast(I32),
        in_=scales[0, 4 * quadrant : 4 * quadrant + 4, :].bitcast(I32),
    )


def tile_list_meet_timestable_levelled_tabled_kernel(
    tc, xt_words, xt_scales, wa_words, wa_scales, tf, wb_words, wb_scales, tv, offs, offs2, offs3, offs4, out
):
    nc = tc.nc
    with ExitStack() as ctx:
        sb = ctx.enter_context(tc.tile_pool(name="sb", bufs=1))
        ps = ctx.enter_context(tc.psum_pool(name="ps", bufs=1))

        list_a = sb.tile([P, J // 16], U16, name="list_a")
        list_f = sb.tile([P, J // 16], U16, name="list_f")
        list_b = sb.tile([P, I // 16], U16, name="list_b")
        list_v = sb.tile([P, I // 16], U16, name="list_v")
        xt_w = sb.tile([P, T], U32, name="xt_w", align_bytes=64)
        xt_s = sb.tile([P, T], U8, name="xt_s", align_bytes=64)
        wa_w_raw = sb.tile([P, R], U32, name="wa_w_raw", align_bytes=64)
        wa_s_raw = sb.tile([P, R], U8, name="wa_s_raw", align_bytes=64)
        wb_w_raw = sb.tile([P, 2 * R], U8, name="wb_w_raw", align_bytes=64)
        wb_s_raw = sb.tile([P, R], U8, name="wb_s_raw", align_bytes=64)
        tf_rows = [sb.tile([P, C], F32, name="tf_rows%d" % t) for t in range(PACK)]
        tv_rows = sb.tile([P, J // P, Q], F32, name="tv_rows")


        for plane in (xt_s, wb_s_raw, wa_s_raw):
            nc.vector.memset(plane[:].bitcast(I32), 0)

        nc.sync.dma_start(list_b[:], offs3)
        nc.scalar.dma_start(out=wb_w_raw[:].bitcast(I32), in_=wb_words[0].bitcast(I32))
        nc.sync.dma_start(list_a[:], offs)
        tf_dealt = tf.rearrange("(b t u) c -> t b u c", t=PACK, u=RUN)
        for quadrant in range(4):
            load_scale_rows(nc.sync if quadrant % 2 else nc.scalar, xt_s, xt_scales, quadrant)
        nc.scalar.dma_start(
            out=xt_w[:].bitcast(I32), in_=xt_words[0].rearrange("p c r -> p (c r)").bitcast(I32)
        )
        for t in range(2):
            nc.gpsimd.dma_start(out=tf_rows[t][:], in_=tf_dealt[t])
        for quadrant in range(4):
            load_scale_rows(nc.scalar if quadrant % 2 else nc.sync, wb_s_raw, wb_scales, quadrant)
        nc.sync.dma_start(list_f[:], offs2)
        nc.sync.dma_start(
            out=wa_w_raw[:].bitcast(I32), in_=wa_words[0].rearrange("p c r -> p (c r)").bitcast(I32)
        )
        for quadrant in range(4):
            load_scale_rows(nc.sync, wa_s_raw, wa_scales, quadrant)
        for t in range(2, PACK):
            nc.sync.dma_start(out=tf_rows[t][:], in_=tf_dealt[t])
        nc.sync.dma_start(out=tv_rows[:], in_=tv.rearrange("(h p) q -> p h q", p=P))
        nc.sync.dma_start(list_v[:], offs4)

        xb_w = sb.tile([P, I], U32, name="xb_w", align_bytes=64)
        xb_s = sb.tile([P, I], U8, name="xb_s", align_bytes=64)
        xa_w = sb.tile([P, J], U32, name="xa_w", align_bytes=64)
        xa_s = sb.tile([P, J], U8, name="xa_s", align_bytes=64)

        wb_w = sb.tile([P, 2 * R], U8, name="wb_w", align_bytes=64)
        wb_s = sb.tile([P, R], U8, name="wb_s", align_bytes=64)
        wa_w = sb.tile([P, R], U32, name="wa_w", align_bytes=64)
        wa_s = sb.tile([P, R], U8, name="wa_s", align_bytes=64)

        def deal(copy, dst, src):
            copy(
                out=dst[:].bitcast(U32).rearrange("p (t b w) -> p t b w", t=PACK, b=R // 32),
                in_=src[:].bitcast(U32).rearrange("p (b t w) -> p t b w", t=PACK, b=R // 32),
            )

        def first_stage(name, w, w_dtype, bytes_per_column, s, x_w, x_s):
            banks = [ps.tile([P, PACK, HALF], F32, name="%s%d" % (name, h)) for h in range(2)]
            for h in range(2):
                cols = slice(h * HALF, (h + 1) * HALF)
                for t in range(PACK):
                    nc.tensor.matmul_mx(
                        out=banks[h][:, t, :],
                        lhsT=w[:, t * P * bytes_per_column : (t + 1) * P * bytes_per_column].bitcast(w_dtype),
                        lhsT_scale=s[:, t * P : (t + 1) * P],
                        rhs=x_w[:, cols].bitcast(E4M3),
                        rhs_scale=x_s[:, cols],
                        start=True,
                        stop=True,
                    )
            return banks

        nc.vector.tensor_copy(xb_s[:], xt_s[:].indirect(list_b[:]))
        nc.vector.tensor_copy(xa_s[:], xt_s[:].indirect(list_a[:]))
        nc.vector.tensor_copy(xb_w[:], xt_w[:].indirect(list_b[:]))
        nc.vector.tensor_copy(xa_w[:], xt_w[:].indirect(list_a[:]))
        deal(nc.scalar.copy, wb_w, wb_w_raw)
        deal(nc.scalar.copy, wb_s, wb_s_raw)
        zb = first_stage("zb", wb_w, E2M1, 2, wb_s, xb_w, xb_s)
        deal(nc.scalar.copy, wa_w, wa_w_raw)

        tf_g = sb.tile([P, PACK, J], F32, name="tf_g")
        for t in range(PACK):
            nc.scalar.activation(tf_g[:, t, :], tf_rows[t][:].indirect(list_f[:]), ACT.Copy)
        tv_g = [sb.tile([P, I], F32, name="tv_g%d" % h) for h in range(2)]
        for h in range(2):
            nc.scalar.activation(tv_g[h][:], tv_rows[:, h, :].indirect(list_v[:]), ACT.Copy)

        groups = HALF // BUNDLE
        sums = [sb.tile([P, groups, PACK], F32, name="sums%d" % h) for h in range(2)]
        means = [sb.tile([P, groups, PACK], F32, name="means%d" % h) for h in range(2)]
        hb = sb.tile([P, I, PACK], BF16, name="hb", align_bytes=64)
        for h in range(2):
            nc.vector.tensor_reduce(
                out=sums[h][:],
                in_=zb[h][:].rearrange("p t (g u) -> p g t u", u=BUNDLE),
                axis=mybir.AxisListType.X,
                op=ALU.add,
            )

        def take_mean(h):
            nc.gpsimd.tensor_scalar(
                out=means[h][:], in0=sums[h][:], scalar1=1.0 / BUNDLE, scalar2=0.0, op0=ALU.mult, op1=ALU.add
            )

        take_mean(0)
        deal(nc.gpsimd.tensor_copy, wa_s, wa_s_raw)
        take_mean(1)
        za = first_stage("za", wa_w, E5M2, 1, wa_s, xa_w, xa_s)
        for h in range(2):
            nc.vector.tensor_tensor(
                out=hb[:, h * HALF : (h + 1) * HALF, :].rearrange("p (g u) t -> p g u t", u=BUNDLE),
                in0=zb[h][:].rearrange("p t (g u) -> p g u t", u=BUNDLE),
                in1=means[h][:].unsqueeze(2).to_broadcast([P, groups, BUNDLE, PACK]),
                op=ALU.subtract,
            )

        ha = [sb.tile([P, HALF, PACK], BF16, name="ha%d" % h, align_bytes=64) for h in range(2)]
        ha_w = [sb.tile([P, HALF], U32, name="ha_w%d" % h, align_bytes=64) for h in range(2)]
        ha_s = [sb.tile([P, HALF], U8, name="ha_s%d" % h, align_bytes=64) for h in range(2)]
        hb_w = sb.tile([P, I], U32, name="hb_w", align_bytes=64)
        hb_s = sb.tile([P, I], U8, name="hb_s", align_bytes=64)

        def scale_rows(h):
            nc.vector.tensor_tensor(
                out=ha[h][:].rearrange("p (c i) t -> p c t i", i=4),
                in0=za[h][:].rearrange("p t (c i) -> p c t i", i=4),
                in1=tf_g[:, :, h * HALF : (h + 1) * HALF].rearrange("p t (c i) -> p c t i", i=4),
                op=ALU.mult,
            )

        def quantize_rows(h):
            nc.vector.quantize_mx(
                out=ha_w[h][:].bitcast(E4M3), scales=ha_s[h][:], in_=ha[h][:].rearrange("p j t -> p (j t)")
            )

        def quantize_columns(h):
            cols = slice(h * HALF, (h + 1) * HALF)
            nc.vector.quantize_mx(
                out=hb_w[:, cols].bitcast(E5M2),
                scales=hb_s[:, cols],
                in_=hb[:, cols, :].rearrange("p i t -> p (i t)"),
            )

        quantize_columns(0)
        scale_rows(0)
        quantize_columns(1)
        quantize_rows(0)
        scale_rows(1)
        quantize_rows(1)

        for h in range(2):
            for c in range(2):
                cols = slice(c * HALF, (c + 1) * HALF)
                scores = ps.tile([P, HALF], F32, name="scores%d%d" % (h, c))
                nc.tensor.matmul_mx(
                    out=scores[:],
                    lhsT=ha_w[h][:].bitcast(E4M3),
                    lhsT_scale=ha_s[h][:],
                    rhs=hb_w[:, cols].bitcast(E5M2),
                    rhs_scale=hb_s[:, cols],
                    start=True,
                    stop=True,
                )
                squashed = sb.tile([P, HALF], F32, name="squashed%d%d" % (h, c))
                nc.scalar.activation(squashed[:], scores[:], ACT.Tanh, scale=0.04)
                result = sb.tile([P, HALF], F32, name="result%d%d" % (h, c))
                nc.vector.tensor_tensor(out=result[:], in0=squashed[:], in1=tv_g[h][:, cols], op=ALU.mult)
                nc.sync.dma_start(out=out[h * P : (h + 1) * P, cols], in_=result[:])
